import numpy as np
import ml_dtypes


def mxq(x, axis, fmt="e4m3"):
    dtype, down = {"e4m3": (ml_dtypes.float8_e4m3fn, 7), "e5m2": (ml_dtypes.float8_e5m2, 14)}[fmt]
    v = np.moveaxis(np.asarray(x, np.float32).astype(ml_dtypes.bfloat16).astype(np.float64), axis, -1)
    blocks = v.reshape(v.shape[:-1] + (-1, 32))
    amax = np.abs(blocks).max(-1, keepdims=True)
    byte = np.maximum(np.where(amax > 0, np.frexp(amax)[1] - 1 + 127, 0) - down, 1)
    scale = np.exp2(byte - 127.0)
    codes = (blocks / scale).astype(np.float32).astype(dtype).astype(np.float64)
    return np.moveaxis((codes * scale).reshape(v.shape), -1, axis)


WIDE = False


def mx_kscale(k, group=512):
    if not WIDE:
        return np.ones(k)
    levels = np.array([10, -10, 5, -5, 0])
    if group != 512:
        return np.exp2(np.random.permutation(np.resize(levels, k // group))).repeat(group)
    if k % 512:
        return np.exp2(np.random.permutation(np.resize(levels, k // 32))).repeat(32)
    a = np.empty((k // 512, 16))
    for p in range(k // 512):
        a[p, :8] = np.random.permutation(np.resize(levels, 8))
        for g in range(8):
            far = levels[np.abs(levels - a[p, g]) >= 10]
            a[p, g + 8] = far[np.random.randint(len(far))]
    return np.exp2(a.ravel()).repeat(32)


def f64(x):
    return np.asarray(x).astype(np.float64)


def striped(idx):
    return np.tile(np.asarray(idx).reshape(-1, 16).T, (8, 1)).astype(np.uint16)


def unstriped(offs):
    return offs[:16].T.reshape(-1).astype(np.int64)


H, KV, D, NQ, N = 4, 4, 256, 512, 512
CAP = 2.0


def setup_inputs():
    n = np.random.standard_normal
    s = mx_kscale(D, 0)[:, None]
    u = mx_kscale(N)
    t = np.random.uniform(0.5, 2.0, N) * u
    v = n((KV, N, 128))
    return {
        "qT": (n((H, D, NQ)) * s * (0.70 / np.sqrt(D))).astype(np.float32),
        "kT": (n((KV, D, N)) / s).astype(np.float32),
        "t": t.reshape(N, 1).astype(np.float32),
        "v": (v / t[:, None]).astype(np.float32),
        "kb": (0.5 * n((N, 1))).astype(np.float32),
    }


def reference(qT, kT, t, v, kb):
    a = mxq(f64(kT), 1, "e4m3").transpose(0, 2, 1) @ mxq(f64(qT), 1, "e4m3")
    a = a + f64(kb)
    a = CAP * np.tanh(a / CAP)
    p = 1.0 / (1.0 + np.exp(-a))
    w = p * f64(t)
    y = mxq(w, 1, "e4m3").transpose(0, 2, 1) @ mxq(f64(v), 1, "e4m3")
    y = y / 16.0
    return y

@@ -1,0 +1,284 @@
+from contextlib import ExitStack
+
+import concourse.mybir as mybir
+
+H, D, NQ, N, E = 4, 256, 512, 512, 128
+FLOPS = 2 * H * NQ * N * (D + E)
+
+F32 = mybir.dt.float32
+BF16 = mybir.dt.bfloat16
+U32 = mybir.dt.uint32
+U8 = mybir.dt.uint8
+FP8X4 = mybir.dt.float8_e4m3fn_x4
+ACT = mybir.ActivationFunctionType
+ALU = mybir.AluOpType
+
+P = 128
+PACK = 4
+ROWS = D // PACK
+CH = 128
+SCORE_BANKS = 3
+
+
+def tile_rows_a_sigmoid_kb_cap_kernel(tc, qT, kT, t, v, kb, out):
+    nc = tc.nc
+    with ExitStack() as ctx:
+        sb = ctx.enter_context(tc.tile_pool(name="sb", bufs=1))
+        ps = ctx.enter_context(tc.psum_pool(name="ps", bufs=1))
+        ctx.enter_context(tc.manual_schedule())
+
+        def new(name, shape, dtype):
+            return sb.tile(shape, dtype, name=name, align_bytes=64)
+
+        score_bank = [[ps.tile([P, 512], F32, name="score%d_%d" % (g, b)) for b in range(SCORE_BANKS)] for g in range(2)]
+        out_bank = [ps.tile([P, 512], F32, name="y%d" % b) for b in range(2)]
+        bank_turn = [0, 0]
+
+        def pair_rows(x, g):
+            return x[2 * g : 2 * g + 2].rearrange("h (p j) n -> (h p) j n", j=PACK)
+
+        raw = {}
+
+        def load(name, src):
+            raw[name] = new("raw_" + name, list(src.shape), F32)
+            nc.sync.dma_start(out=raw[name][:], in_=src)
+
+        t_col = new("t_col", [P, PACK], F32)
+        kb_col = new("kb_col", [P, PACK], F32)
+        kb_half = new("kb_half", [P, PACK], F32)
+        warm = new("warm", [P, 1], F32)
+        warm_out = new("warm_out", [P, 1], F32)
+
+        k_bf = [new("k_bf%d" % g, [P, PACK, P, PACK], BF16) for g in range(2)]
+        q_bf = [new("q_bf%d" % g, [P, NQ, PACK], BF16) for g in range(2)]
+        v_bf = [new("v_bf%d" % g, [P, 2, E, PACK], BF16) for g in range(2)]
+        codes = {}
+        scales = {}
+
+        def copy(engine, dst, src):
+            if engine == "V":
+                nc.vector.tensor_copy(out=dst, in_=src)
+            else:
+                nc.scalar.copy(out=dst, in_=src)
+
+        def cast_k(engine, g, name, s0, a, b):
+            copy(engine,
+                 k_bf[g][:, :, s0 + a : s0 + b, :].rearrange("p r s j -> p s j r"),
+                 raw[name][:, :, PACK * a : PACK * b].rearrange("p j (s r) -> p s j r", r=PACK))
+
+        def cast_q(engine, g, name, q0, a, b):
+            copy(engine,
+                 q_bf[g][:, q0 + a : q0 + b, :].rearrange("p (c i) j -> p c j i", i=2),
+                 raw[name][:, :, a:b].rearrange("p j (c i) -> p c j i", i=2))
+
+        def cast_v(engine, h):
+            copy(engine,
+                 v_bf[h // 2][:, h % 2].rearrange("p (c i) j -> p c j i", i=2),
+                 raw["v%d" % (h // 2)][:, h % 2].rearrange("p j (c i) -> p c j i", i=2))
+
+        def quantize(name, src, width):
+            cd = new("codes_" + name, [P, width], U32)
+            sc = new("scales_" + name, [P, width], U8)
+            nc.vector.quantize_mx(out=cd[:].bitcast(FP8X4), scales=sc[:], in_=src)
+            return cd, sc
+
+        def quant_k(g, r0, r1):
+            cd, sc = quantize("k%d_%d" % (g, r0), k_bf[g][:, r0:r1].rearrange("p r s j -> p (r s j)"), (r1 - r0) * P)
+            for r in range(r0, r1):
+                codes["k", g, r] = cd[:, (r - r0) * P : (r - r0 + 1) * P]
+                scales["k", g, r] = sc[:, (r - r0) * P : (r - r0 + 1) * P]
+
+        def quant_q(g, c0, c1):
+            cd, sc = quantize("q%d_%d" % (g, c0), q_bf[g][:, c0 * CH : c1 * CH].rearrange("p q j -> p (q j)"), (c1 - c0) * CH)
+            for c in range(c0, c1):
+                codes["q", g, c] = cd[:, (c - c0) * CH : (c - c0 + 1) * CH]
+                scales["q", g, c] = sc[:, (c - c0) * CH : (c - c0 + 1) * CH]
+
+        def quant_v(g):
+            cd, sc = quantize("v%d" % g, v_bf[g][:].rearrange("p h e j -> p (h e j)"), 2 * E)
+            for x in range(2):
+                codes["v", 2 * g + x] = cd[:, x * E : (x + 1) * E]
+                scales["v", 2 * g + x] = sc[:, x * E : (x + 1) * E]
+
+        capped = {}
+        prob = {}
+        w_bf = {}
+
+        def scores(h, c0, c1, r0, r1):
+            g, x = divmod(h, 2)
+            rows = slice(ROWS * x, ROWS * (x + 1))
+            nq = (c1 - c0) * CH
+            if (h, c0) not in capped:
+                u = new("u%d_%d" % (h, c0), [P, PACK, nq], F32)
+                for c in range(c0, c1):
+                    capped[h, c] = (u, c0)
+            u = capped[h, c0][0]
+            bank = score_bank[x][bank_turn[x] % SCORE_BANKS]
+            bank_turn[x] = bank_turn[x] + 1
+            for r in range(r0, r1):
+                for c in range(c0, c1):
+                    col = (r - r0) * nq + (c - c0) * CH
+                    nc.tensor.matmul_mx(
+                        out=bank[:, col : col + CH],
+                        lhsT=codes["k", g, r][rows, :].bitcast(FP8X4),
+                        lhsT_scale=scales["k", g, r][rows, :],
+                        rhs=codes["q", g, c][rows, :].bitcast(FP8X4),
+                        rhs_scale=scales["q", g, c][rows, :],
+                        start=True,
+                        stop=True,
+                    )
+            for r in range(r0, r1):
+                col = (r - r0) * nq
+                nc.scalar.activation(out=u[:, r, :], in_=bank[:, col : col + nq], func=ACT.Tanh,
+                                     bias=kb_half[:, r : r + 1], scale=0.5)
+
+        def sigmoid(h, c0, c1):
+            u, base = capped[h, c0]
+            pr = new("p%d_%d" % (h, c0), [P, PACK, (c1 - c0) * CH], F32)
+            for c in range(c0, c1):
+                prob[h, c] = (pr, c0)
+            nc.scalar.activation(out=pr[:], in_=u[:, :, (c0 - base) * CH : (c1 - base) * CH], func=ACT.Sigmoid, scale=2.0)
+
+        def weigh(h, c0, c1):
+            pr, base = prob[h, c0]
+            nq = (c1 - c0) * CH
+            w = new("w%d_%d" % (h, c0), [P, nq, PACK], BF16)
+            w_bf[h, c0] = w
+            nc.vector.tensor_tensor(
+                out=w[:].rearrange("p (c i) r -> p c r i", i=2),
+                in0=pr[:, :, (c0 - base) * CH : (c1 - base) * CH].rearrange("p r (c i) -> p c r i", i=2),
+                in1=t_col[:].unsqueeze(1).unsqueeze(3).to_broadcast([P, nq // 2, PACK, 2]),
+                op=ALU.mult,
+            )
+
+        def quant_w(h, c0, c1):
+            cd, sc = quantize("w%d_%d" % (h, c0), w_bf[h, c0][:].rearrange("p q r -> p (q r)"), (c1 - c0) * CH)
+            for c in range(c0, c1):
+                codes["w", h, c] = cd[:, (c - c0) * CH : (c - c0 + 1) * CH]
+                scales["w", h, c] = sc[:, (c - c0) * CH : (c - c0 + 1) * CH]
+
+        def values(h, c0, c1, b, base):
+            for c in range(c0, c1):
+                nc.tensor.matmul_mx(
+                    out=out_bank[b][:, (c - base) * E : (c - base + 1) * E],
+                    lhsT=codes["w", h, c].bitcast(FP8X4),
+                    lhsT_scale=scales["w", h, c],
+                    rhs=codes["v", h].bitcast(FP8X4),
+                    rhs_scale=scales["v", h],
+                    start=True,
+                    stop=True,
+                )
+
+        def finish(engine, h, c0, c1, b):
+            n = c1 - c0
+            y = new("y%d_%d" % (h, c0), [P, n * E], F32)
+            if engine == "V":
+                nc.vector.tensor_scalar(out=y[:], in0=out_bank[b][:, : n * E], scalar1=1.0 / 16.0, scalar2=None, op0=ALU.mult)
+            else:
+                nc.scalar.activation(out=y[:], in_=out_bank[b][:, : n * E], func=ACT.Copy, scale=1.0 / 16.0)
+            nc.sync.dma_start(
+                out=out[h, c0 * CH : c1 * CH, :].rearrange("(c m) e -> m c e", m=P),
+                in_=y[:].rearrange("p (c e) -> p c e", e=E),
+            )
+
+        nc.scalar.dma_start(out=kb_col[:], in_=kb.rearrange("(p r) o -> p (r o)", r=PACK))
+        nc.scalar.dma_start(out=t_col[:], in_=t.rearrange("(p r) o -> p (r o)", r=PACK))
+        load("q0a", pair_rows(qT, 0)[:, :, 0:128])
+        load("k0a", pair_rows(kT, 0)[:, :, 0:256])
+        load("k0b", pair_rows(kT, 0)[:, :, 256:512])
+        load("q0b", pair_rows(qT, 0)[:, :, 128:512])
+        load("k1", pair_rows(kT, 1))
+        load("q1", pair_rows(qT, 1))
+        load("v0", v[0:2].rearrange("h (p j) e -> p h j e", j=PACK))
+        load("v1", v[2:4].rearrange("h (p j) e -> p h j e", j=PACK))
+        nc.vector.memset(warm[:], 0.0)
+        nc.scalar.activation(out=warm_out[:], in_=warm[:], func=ACT.Sigmoid)
+        nc.vector.tensor_scalar(out=kb_half[:], in0=kb_col[:], scalar1=0.5, scalar2=None, op0=ALU.mult)
+        cast_q("S", 0, "q0a", 0, 0, 128)
+        cast_k("V", 0, "k0a", 0, 0, 64)
+        cast_k("S", 0, "k0b", 64, 40, 64)
+        cast_k("V", 0, "k0b", 64, 0, 40)
+        quant_q(0, 0, 1)
+        quant_k(0, 1, 2)
+        quant_k(0, 0, 1)
+        scores(1, 0, 1, 1, 2)
+        quant_k(0, 2, 4)
+        cast_q("V", 0, "q0b", 128, 0, 384)
+        scores(0, 0, 1, 1, 2)
+        scores(0, 0, 1, 0, 1)
+        scores(1, 0, 1, 0, 1)
+        quant_q(0, 1, 2)
+        quant_q(0, 2, 4)
+        cast_k("V", 1, "k1", 0, 0, 128)
+        scores(1, 0, 1, 2, 4)
+        scores(0, 0, 1, 2, 4)
+        sigmoid(1, 0, 1)
+        weigh(1, 0, 1)
+        sigmoid(0, 0, 1)
+        scores(0, 1, 4, 2, 3)
+        scores(0, 1, 4, 1, 2)
+        scores(0, 1, 4, 3, 4)
+        scores(1, 1, 4, 2, 3)
+        scores(1, 1, 4, 0, 1)
+        quant_k(1, 0, 4)
+        cast_q("V", 1, "q1", 0, 0, 512)
+        cast_v("V", 1)
+        scores(0, 1, 4, 0, 1)
+        scores(1, 1, 4, 1, 2)
+        cast_v("V", 0)
+        scores(1, 1, 4, 3, 4)
+        sigmoid(0, 1, 2)
+        sigmoid(1, 1, 2)
+        quant_q(1, 0, 4)
+        weigh(0, 1, 2)
+        weigh(0, 0, 1)
+        quant_v(0)
+        sigmoid(0, 2, 4)
+        sigmoid(1, 2, 4)
+        quant_w(0, 0, 1)
+        scores(2, 0, 4, 0, 1)
+        scores(2, 0, 4, 1, 2)
+        quant_w(1, 0, 1)
+        scores(2, 0, 4, 2, 3)
+        scores(2, 0, 4, 3, 4)
+        quant_w(0, 1, 2)
+        scores(3, 0, 2, 0, 2)
+        weigh(1, 1, 2)
+        weigh(0, 2, 4)
+        quant_w(1, 1, 2)
+        sigmoid(2, 0, 2)
+        sigmoid(2, 2, 4)
+        quant_w(0, 2, 4)
+        values(0, 0, 4, 0, 0)
+        weigh(1, 2, 4)
+        cast_v("V", 3)
+        cast_v("V", 2)
+        quant_w(1, 2, 4)
+        scores(3, 0, 2, 2, 4)
+        values(1, 0, 4, 1, 0)
+        scores(3, 2, 4, 2, 4)
+        sigmoid(3, 0, 2)
+        quant_v(1)
+        weigh(2, 0, 2)
+        weigh(2, 2, 4)
+        finish("V", 1, 0, 4, 1)
+        quant_w(2, 0, 2)
+        quant_w(2, 2, 4)
+        scores(3, 2, 4, 0, 2)
+        weigh(3, 0, 2)
+        quant_w(3, 0, 2)
+        finish("S", 0, 0, 4, 0)
+        sigmoid(3, 2, 3)
+        sigmoid(3, 3, 4)
+        values(2, 0, 4, 0, 0)
+        finish("S", 2, 0, 4, 0)
+        weigh(3, 2, 3)
+        weigh(3, 3, 4)
+        values(3, 0, 2, 1, 0)
+        quant_w(3, 2, 3)
+        finish("S", 3, 0, 2, 1)
+        values(3, 2, 3, 0, 2)
+        finish("S", 3, 2, 3, 0)
+        quant_w(3, 3, 4)
+        values(3, 3, 4, 1, 3)
+        finish("S", 3, 3, 4, 1)

@@ -17,7 +17,7 @@ P = 128
 PACK = 4
 ROWS = D // PACK
 CH = 128
-SCORE_BANKS = 3
+SCORE_BANKS = (3, 3)
 
 
 def tile_rows_a_sigmoid_kb_cap_kernel(tc, qT, kT, t, v, kb, out):
@@ -30,7 +30,7 @@ def tile_rows_a_sigmoid_kb_cap_kernel(tc, qT, kT, t, v, kb, out):
         def new(name, shape, dtype):
             return sb.tile(shape, dtype, name=name, align_bytes=64)
 
-        score_bank = [[ps.tile([P, 512], F32, name="score%d_%d" % (g, b)) for b in range(SCORE_BANKS)] for g in range(2)]
+        score_bank = [[ps.tile([P, 512], F32, name="score%d_%d" % (g, b)) for b in range(SCORE_BANKS[g])] for g in range(2)]
         out_bank = [ps.tile([P, 512], F32, name="y%d" % b) for b in range(2)]
         bank_turn = [0, 0]
 
@@ -51,7 +51,7 @@ def tile_rows_a_sigmoid_kb_cap_kernel(tc, qT, kT, t, v, kb, out):
 
         k_bf = [new("k_bf%d" % g, [P, PACK, P, PACK], BF16) for g in range(2)]
         q_bf = [new("q_bf%d" % g, [P, NQ, PACK], BF16) for g in range(2)]
-        v_bf = [new("v_bf%d" % g, [P, 2, E, PACK], BF16) for g in range(2)]
+        v_bf = new("v_bf", [P, H, E, PACK], BF16)
         codes = {}
         scales = {}
 
@@ -71,10 +71,10 @@ def tile_rows_a_sigmoid_kb_cap_kernel(tc, qT, kT, t, v, kb, out):
                  q_bf[g][:, q0 + a : q0 + b, :].rearrange("p (c i) j -> p c j i", i=2),
                  raw[name][:, :, a:b].rearrange("p j (c i) -> p c j i", i=2))
 
-        def cast_v(engine, h):
+        def cast_v(engine, name, h0, h1):
             copy(engine,
-                 v_bf[h // 2][:, h % 2].rearrange("p (c i) j -> p c j i", i=2),
-                 raw["v%d" % (h // 2)][:, h % 2].rearrange("p j (c i) -> p c j i", i=2))
+                 v_bf[:, h0:h1].rearrange("p h (c i) j -> p h c j i", i=2),
+                 raw[name][:].rearrange("p h j (c i) -> p h c j i", i=2))
 
         def quantize(name, src, width):
             cd = new("codes_" + name, [P, width], U32)
@@ -94,41 +94,44 @@ def tile_rows_a_sigmoid_kb_cap_kernel(tc, qT, kT, t, v, kb, out):
                 codes["q", g, c] = cd[:, (c - c0) * CH : (c - c0 + 1) * CH]
                 scales["q", g, c] = sc[:, (c - c0) * CH : (c - c0 + 1) * CH]
 
-        def quant_v(g):
-            cd, sc = quantize("v%d" % g, v_bf[g][:].rearrange("p h e j -> p (h e j)"), 2 * E)
-            for x in range(2):
-                codes["v", 2 * g + x] = cd[:, x * E : (x + 1) * E]
-                scales["v", 2 * g + x] = sc[:, x * E : (x + 1) * E]
+        def quant_v(h0, h1):
+            cd, sc = quantize("v%d" % h0, v_bf[:, h0:h1].rearrange("p h e j -> p (h e j)"), (h1 - h0) * E)
+            for h in range(h0, h1):
+                codes["v", h] = cd[:, (h - h0) * E : (h - h0 + 1) * E]
+                scales["v", h] = sc[:, (h - h0) * E : (h - h0 + 1) * E]
 
         capped = {}
         prob = {}
-        w_bf = {}
+        w_bf = [new("w%d" % h, [P, NQ, PACK], BF16) for h in range(H)]
 
-        def scores(h, c0, c1, r0, r1):
-            g, x = divmod(h, 2)
-            rows = slice(ROWS * x, ROWS * (x + 1))
-            nq = (c1 - c0) * CH
-            if (h, c0) not in capped:
-                u = new("u%d_%d" % (h, c0), [P, PACK, nq], F32)
-                for c in range(c0, c1):
-                    capped[h, c] = (u, c0)
-            u = capped[h, c0][0]
-            bank = score_bank[x][bank_turn[x] % SCORE_BANKS]
-            bank_turn[x] = bank_turn[x] + 1
-            for r in range(r0, r1):
-                for c in range(c0, c1):
-                    col = (r - r0) * nq + (c - c0) * CH
+        def scores(*jobs):
+            passes = []
+            reads = []
+            for h, c0, c1, r0, r1 in jobs:
+                g, x = divmod(h, 2)
+                rows = slice(ROWS * x, ROWS * (x + 1))
+                nq = (c1 - c0) * CH
+                if (h, c0) not in capped:
+                    u = new("u%d_%d" % (h, c0), [P, PACK, nq], F32)
+                    for c in range(c0, c1):
+                        capped[h, c] = (u, c0)
+                bank = score_bank[x][bank_turn[x] % SCORE_BANKS[x]]
+                bank_turn[x] = bank_turn[x] + 1
+                passes.append([(bank, (r - r0) * nq + (c - c0) * CH, rows, ("k", g, r), ("q", g, c))
+                               for r in range(r0, r1) for c in range(c0, c1)])
+                reads.extend([(capped[h, c0][0], r, bank, (r - r0) * nq, nq) for r in range(r0, r1)])
+            for step in zip(*passes):
+                for bank, col, rows, keys, queries in step:
                     nc.tensor.matmul_mx(
                         out=bank[:, col : col + CH],
-                        lhsT=codes["k", g, r][rows, :].bitcast(FP8X4),
-                        lhsT_scale=scales["k", g, r][rows, :],
-                        rhs=codes["q", g, c][rows, :].bitcast(FP8X4),
-                        rhs_scale=scales["q", g, c][rows, :],
+                        lhsT=codes[keys][rows, :].bitcast(FP8X4),
+                        lhsT_scale=scales[keys][rows, :],
+                        rhs=codes[queries][rows, :].bitcast(FP8X4),
+                        rhs_scale=scales[queries][rows, :],
                         start=True,
                         stop=True,
                     )
-            for r in range(r0, r1):
-                col = (r - r0) * nq
+            for u, r, bank, col, nq in reads:
                 nc.scalar.activation(out=u[:, r, :], in_=bank[:, col : col + nq], func=ACT.Tanh,
                                      bias=kb_half[:, r : r + 1], scale=0.5)
 
@@ -142,17 +145,15 @@ def tile_rows_a_sigmoid_kb_cap_kernel(tc, qT, kT, t, v, kb, out):
         def weigh(h, c0, c1):
             pr, base = prob[h, c0]
             nq = (c1 - c0) * CH
-            w = new("w%d_%d" % (h, c0), [P, nq, PACK], BF16)
-            w_bf[h, c0] = w
             nc.vector.tensor_tensor(
-                out=w[:].rearrange("p (c i) r -> p c r i", i=2),
+                out=w_bf[h][:, c0 * CH : c1 * CH].rearrange("p (c i) r -> p c r i", i=2),
                 in0=pr[:, :, (c0 - base) * CH : (c1 - base) * CH].rearrange("p r (c i) -> p c r i", i=2),
                 in1=t_col[:].unsqueeze(1).unsqueeze(3).to_broadcast([P, nq // 2, PACK, 2]),
                 op=ALU.mult,
             )
 
         def quant_w(h, c0, c1):
-            cd, sc = quantize("w%d_%d" % (h, c0), w_bf[h, c0][:].rearrange("p q r -> p (q r)"), (c1 - c0) * CH)
+            cd, sc = quantize("w%d_%d" % (h, c0), w_bf[h][:, c0 * CH : c1 * CH].rearrange("p q r -> p (q r)"), (c1 - c0) * CH)
             for c in range(c0, c1):
                 codes["w", h, c] = cd[:, (c - c0) * CH : (c - c0 + 1) * CH]
                 scales["w", h, c] = sc[:, (c - c0) * CH : (c - c0 + 1) * CH]
@@ -169,116 +170,95 @@ def tile_rows_a_sigmoid_kb_cap_kernel(tc, qT, kT, t, v, kb, out):
                     stop=True,
                 )
 
-        def finish(engine, h, c0, c1, b):
+        def finish(engine, h, c0, c1, b, queue=None):
             n = c1 - c0
             y = new("y%d_%d" % (h, c0), [P, n * E], F32)
             if engine == "V":
                 nc.vector.tensor_scalar(out=y[:], in0=out_bank[b][:, : n * E], scalar1=1.0 / 16.0, scalar2=None, op0=ALU.mult)
             else:
                 nc.scalar.activation(out=y[:], in_=out_bank[b][:, : n * E], func=ACT.Copy, scale=1.0 / 16.0)
-            nc.sync.dma_start(
+            (queue or nc.sync).dma_start(
                 out=out[h, c0 * CH : c1 * CH, :].rearrange("(c m) e -> m c e", m=P),
                 in_=y[:].rearrange("p (c e) -> p c e", e=E),
             )
 
         nc.scalar.dma_start(out=kb_col[:], in_=kb.rearrange("(p r) o -> p (r o)", r=PACK))
-        nc.scalar.dma_start(out=t_col[:], in_=t.rearrange("(p r) o -> p (r o)", r=PACK))
-        load("q0a", pair_rows(qT, 0)[:, :, 0:128])
-        load("k0a", pair_rows(kT, 0)[:, :, 0:256])
-        load("k0b", pair_rows(kT, 0)[:, :, 256:512])
-        load("q0b", pair_rows(qT, 0)[:, :, 128:512])
-        load("k1", pair_rows(kT, 1))
-        load("q1", pair_rows(qT, 1))
-        load("v0", v[0:2].rearrange("h (p j) e -> p h j e", j=PACK))
-        load("v1", v[2:4].rearrange("h (p j) e -> p h j e", j=PACK))
         nc.vector.memset(warm[:], 0.0)
         nc.scalar.activation(out=warm_out[:], in_=warm[:], func=ACT.Sigmoid)
+        load("k0", pair_rows(kT, 0))
+        load("q0a", pair_rows(qT, 0)[:, :, 0:128])
+        load("q0b", pair_rows(qT, 0)[:, :, 128:512])
+        nc.sync.dma_start(out=t_col[:], in_=t.rearrange("(p r) o -> p (r o)", r=PACK))
+        load("k1", pair_rows(kT, 1))
+        load("q1", pair_rows(qT, 1))
+        load("va", v[0:2].rearrange("h (p j) e -> p h j e", j=PACK))
+        load("vb", v[2:4].rearrange("h (p j) e -> p h j e", j=PACK))
         nc.vector.tensor_scalar(out=kb_half[:], in0=kb_col[:], scalar1=0.5, scalar2=None, op0=ALU.mult)
-        cast_q("S", 0, "q0a", 0, 0, 128)
-        cast_k("V", 0, "k0a", 0, 0, 64)
-        cast_k("S", 0, "k0b", 64, 40, 64)
-        cast_k("V", 0, "k0b", 64, 0, 40)
+        cast_k("V", 0, "k0", 0, 0, 88)
+        cast_k("S", 0, "k0", 0, 88, 128)
+        cast_q("V", 0, "q0a", 0, 0, 128)
+        quant_k(0, 0, 1)
         quant_q(0, 0, 1)
         quant_k(0, 1, 2)
-        quant_k(0, 0, 1)
-        scores(1, 0, 1, 1, 2)
         quant_k(0, 2, 4)
-        cast_q("V", 0, "q0b", 128, 0, 384)
-        scores(0, 0, 1, 1, 2)
-        scores(0, 0, 1, 0, 1)
-        scores(1, 0, 1, 0, 1)
+        scores((0, 0, 1, 0, 1), (1, 0, 1, 0, 1))
+        scores((0, 0, 1, 1, 2), (1, 0, 1, 1, 2))
+        scores((0, 0, 1, 2, 4), (1, 0, 1, 2, 4))
+        cast_q("V", 0, "q0b", 128, 0, 128)
+        cast_q("V", 0, "q0b", 128, 128, 384)
         quant_q(0, 1, 2)
         quant_q(0, 2, 4)
-        cast_k("V", 1, "k1", 0, 0, 128)
-        scores(1, 0, 1, 2, 4)
-        scores(0, 0, 1, 2, 4)
-        sigmoid(1, 0, 1)
-        weigh(1, 0, 1)
         sigmoid(0, 0, 1)
-        scores(0, 1, 4, 2, 3)
-        scores(0, 1, 4, 1, 2)
-        scores(0, 1, 4, 3, 4)
-        scores(1, 1, 4, 2, 3)
-        scores(1, 1, 4, 0, 1)
-        quant_k(1, 0, 4)
-        cast_q("V", 1, "q1", 0, 0, 512)
-        cast_v("V", 1)
-        scores(0, 1, 4, 0, 1)
-        scores(1, 1, 4, 1, 2)
-        cast_v("V", 0)
-        scores(1, 1, 4, 3, 4)
-        sigmoid(0, 1, 2)
-        sigmoid(1, 1, 2)
-        quant_q(1, 0, 4)
-        weigh(0, 1, 2)
+        sigmoid(1, 0, 1)
+        scores((0, 1, 4, 0, 1), (1, 1, 4, 0, 1))
+        scores((0, 1, 4, 1, 2), (1, 1, 4, 1, 2))
+        scores((0, 1, 4, 2, 3), (1, 1, 4, 2, 3))
+        scores((0, 1, 4, 3, 4), (1, 1, 4, 3, 4))
         weigh(0, 0, 1)
-        quant_v(0)
-        sigmoid(0, 2, 4)
-        sigmoid(1, 2, 4)
-        quant_w(0, 0, 1)
-        scores(2, 0, 4, 0, 1)
-        scores(2, 0, 4, 1, 2)
-        quant_w(1, 0, 1)
-        scores(2, 0, 4, 2, 3)
-        scores(2, 0, 4, 3, 4)
-        quant_w(0, 1, 2)
-        scores(3, 0, 2, 0, 2)
-        weigh(1, 1, 2)
-        weigh(0, 2, 4)
-        quant_w(1, 1, 2)
+        cast_k("V", 1, "k1", 0, 0, 128)
+        weigh(1, 0, 1)
+        cast_q("V", 1, "q1", 0, 0, 512)
+        quant_k(1, 0, 4)
+        quant_q(1, 0, 4)
+        sigmoid(0, 1, 4)
+        sigmoid(1, 1, 4)
+        cast_v("V", "va", 0, 2)
+        cast_v("V", "vb", 2, 4)
+        weigh(0, 1, 4)
+        quant_v(0, 4)
+        quant_w(0, 0, 4)
+        scores((2, 0, 4, 0, 1),)
+        scores((2, 0, 4, 1, 2),)
+        scores((2, 0, 4, 2, 3), (3, 0, 2, 0, 2))
+        scores((2, 0, 4, 3, 4), (3, 0, 2, 2, 4))
+        values(0, 0, 4, 0, 0)
+        weigh(1, 1, 4)
+        finish("V", 0, 0, 4, 0)
+        quant_w(1, 0, 4)
         sigmoid(2, 0, 2)
         sigmoid(2, 2, 4)
-        quant_w(0, 2, 4)
-        values(0, 0, 4, 0, 0)
-        weigh(1, 2, 4)
-        cast_v("V", 3)
-        cast_v("V", 2)
-        quant_w(1, 2, 4)
-        scores(3, 0, 2, 2, 4)
-        values(1, 0, 4, 1, 0)
-        scores(3, 2, 4, 2, 4)
         sigmoid(3, 0, 2)
-        quant_v(1)
+        scores((3, 2, 4, 0, 2),)
+        scores((3, 2, 4, 2, 4),)
+        values(1, 0, 4, 1, 0)
         weigh(2, 0, 2)
         weigh(2, 2, 4)
-        finish("V", 1, 0, 4, 1)
         quant_w(2, 0, 2)
-        quant_w(2, 2, 4)
-        scores(3, 2, 4, 0, 2)
         weigh(3, 0, 2)
-        quant_w(3, 0, 2)
-        finish("S", 0, 0, 4, 0)
+        quant_w(2, 2, 4)
+        finish("S", 1, 0, 4, 1)
         sigmoid(3, 2, 3)
         sigmoid(3, 3, 4)
         values(2, 0, 4, 0, 0)
+        quant_w(3, 0, 2)
+        values(3, 0, 2, 1, 0)
         finish("S", 2, 0, 4, 0)
+        finish("S", 3, 0, 2, 1)
         weigh(3, 2, 3)
         weigh(3, 3, 4)
-        values(3, 0, 2, 1, 0)
         quant_w(3, 2, 3)
-        finish("S", 3, 0, 2, 1)
-        values(3, 2, 3, 0, 2)
-        finish("S", 3, 2, 3, 0)
         quant_w(3, 3, 4)
+        values(3, 2, 3, 0, 2)
         values(3, 3, 4, 1, 3)
-        finish("S", 3, 3, 4, 1)
+        finish("V", 3, 2, 3, 0)
+        finish("S", 3, 3, 4, 1, nc.scalar)

@@ -44,6 +44,7 @@ def tile_rows_a_sigmoid_kb_cap_kernel(tc, qT, kT, t, v, kb, out):
             nc.sync.dma_start(out=raw[name][:], in_=src)
 
         t_col = new("t_col", [P, PACK], F32)
+        t_rep = new("t_rep", [P, PACK, 4], F32)
         kb_col = new("kb_col", [P, PACK], F32)
         kb_half = new("kb_half", [P, PACK], F32)
         warm = new("warm", [P, 1], F32)
@@ -68,13 +69,13 @@ def tile_rows_a_sigmoid_kb_cap_kernel(tc, qT, kT, t, v, kb, out):
 
         def cast_q(engine, g, name, q0, a, b):
             copy(engine,
-                 q_bf[g][:, q0 + a : q0 + b, :].rearrange("p (c i) j -> p c j i", i=2),
-                 raw[name][:, :, a:b].rearrange("p j (c i) -> p c j i", i=2))
+                 q_bf[g][:, q0 + a : q0 + b, :].rearrange("p (c i) j -> p c j i", i=4),
+                 raw[name][:, :, a:b].rearrange("p j (c i) -> p c j i", i=4))
 
         def cast_v(engine, name, h0, h1):
             copy(engine,
-                 v_bf[:, h0:h1].rearrange("p h (c i) j -> p h c j i", i=2),
-                 raw[name][:].rearrange("p h j (c i) -> p h c j i", i=2))
+                 v_bf[:, h0:h1].rearrange("p h (c i) j -> p h c j i", i=4),
+                 raw[name][:].rearrange("p h j (c i) -> p h c j i", i=4))
 
         def quantize(name, src, width):
             cd = new("codes_" + name, [P, width], U32)
@@ -146,9 +147,9 @@ def tile_rows_a_sigmoid_kb_cap_kernel(tc, qT, kT, t, v, kb, out):
             pr, base = prob[h, c0]
             nq = (c1 - c0) * CH
             nc.vector.tensor_tensor(
-                out=w_bf[h][:, c0 * CH : c1 * CH].rearrange("p (c i) r -> p c r i", i=2),
-                in0=pr[:, :, (c0 - base) * CH : (c1 - base) * CH].rearrange("p r (c i) -> p c r i", i=2),
-                in1=t_col[:].unsqueeze(1).unsqueeze(3).to_broadcast([P, nq // 2, PACK, 2]),
+                out=w_bf[h][:, c0 * CH : c1 * CH].rearrange("p (c i) r -> p c r i", i=4),
+                in0=pr[:, :, (c0 - base) * CH : (c1 - base) * CH].rearrange("p r (c i) -> p c r i", i=4),
+                in1=t_rep[:].unsqueeze(1).to_broadcast([P, nq // 4, PACK, 4]),
                 op=ALU.mult,
             )
 
@@ -170,13 +171,13 @@ def tile_rows_a_sigmoid_kb_cap_kernel(tc, qT, kT, t, v, kb, out):
                     stop=True,
                 )
 
-        def finish(engine, h, c0, c1, b, queue=None):
+        def finish(engine, h, c0, c1, b, base, queue=None):
             n = c1 - c0
             y = new("y%d_%d" % (h, c0), [P, n * E], F32)
             if engine == "V":
-                nc.vector.tensor_scalar(out=y[:], in0=out_bank[b][:, : n * E], scalar1=1.0 / 16.0, scalar2=None, op0=ALU.mult)
+                nc.vector.tensor_scalar(out=y[:], in0=out_bank[b][:, (c0 - base) * E : (c1 - base) * E], scalar1=1.0 / 16.0, scalar2=None, op0=ALU.mult)
             else:
-                nc.scalar.activation(out=y[:], in_=out_bank[b][:, : n * E], func=ACT.Copy, scale=1.0 / 16.0)
+                nc.scalar.activation(out=y[:], in_=out_bank[b][:, (c0 - base) * E : (c1 - base) * E], func=ACT.Copy, scale=1.0 / 16.0)
             (queue or nc.sync).dma_start(
                 out=out[h, c0 * CH : c1 * CH, :].rearrange("(c m) e -> m c e", m=P),
                 in_=y[:].rearrange("p (c e) -> p c e", e=E),
@@ -207,6 +208,7 @@ def tile_rows_a_sigmoid_kb_cap_kernel(tc, qT, kT, t, v, kb, out):
         cast_q("V", 0, "q0b", 128, 0, 128)
         cast_q("V", 0, "q0b", 128, 128, 384)
         quant_q(0, 1, 2)
+        nc.vector.tensor_copy(out=t_rep[:], in_=t_col[:].unsqueeze(2).to_broadcast([P, PACK, 4]))
         quant_q(0, 2, 4)
         sigmoid(0, 0, 1)
         sigmoid(1, 0, 1)
@@ -233,7 +235,7 @@ def tile_rows_a_sigmoid_kb_cap_kernel(tc, qT, kT, t, v, kb, out):
         scores((2, 0, 4, 3, 4), (3, 0, 2, 2, 4))
         values(0, 0, 4, 0, 0)
         weigh(1, 1, 4)
-        finish("V", 0, 0, 4, 0)
+        finish("V", 0, 0, 4, 0, 0)
         quant_w(1, 0, 4)
         sigmoid(2, 0, 2)
         sigmoid(2, 2, 4)
@@ -246,19 +248,19 @@ def tile_rows_a_sigmoid_kb_cap_kernel(tc, qT, kT, t, v, kb, out):
         quant_w(2, 0, 2)
         weigh(3, 0, 2)
         quant_w(2, 2, 4)
-        finish("S", 1, 0, 4, 1)
+        finish("S", 1, 0, 4, 1, 0)
         sigmoid(3, 2, 3)
         sigmoid(3, 3, 4)
         values(2, 0, 4, 0, 0)
         quant_w(3, 0, 2)
         values(3, 0, 2, 1, 0)
-        finish("S", 2, 0, 4, 0)
-        finish("S", 3, 0, 2, 1)
+        finish("S", 2, 0, 4, 0, 0)
+        finish("S", 3, 0, 2, 1, 0)
         weigh(3, 2, 3)
         weigh(3, 3, 4)
         quant_w(3, 2, 3)
         quant_w(3, 3, 4)
         values(3, 2, 3, 0, 2)
         values(3, 3, 4, 1, 3)
-        finish("V", 3, 2, 3, 0)
-        finish("S", 3, 3, 4, 1, nc.scalar)
+        finish("V", 3, 2, 3, 0, 2)
+        finish("S", 3, 3, 4, 1, 3, nc.scalar)

from contextlib import ExitStack

import concourse.mybir as mybir

H, D, NQ, N, E = 4, 256, 512, 512, 128
FLOPS = 2 * H * NQ * N * (D + E)

F32 = mybir.dt.float32
BF16 = mybir.dt.bfloat16
U32 = mybir.dt.uint32
U8 = mybir.dt.uint8
FP8X4 = mybir.dt.float8_e4m3fn_x4
ACT = mybir.ActivationFunctionType
ALU = mybir.AluOpType

P = 128
PACK = 4
ROWS = D // PACK
CH = 128
SCORE_BANKS = (3, 3)


def tile_rows_a_sigmoid_kb_cap_kernel(tc, qT, kT, t, v, kb, out):
    nc = tc.nc
    with ExitStack() as ctx:
        sb = ctx.enter_context(tc.tile_pool(name="sb", bufs=1))
        ps = ctx.enter_context(tc.psum_pool(name="ps", bufs=1))
        ctx.enter_context(tc.manual_schedule())

        def new(name, shape, dtype):
            return sb.tile(shape, dtype, name=name, align_bytes=64)

        score_bank = [[ps.tile([P, 512], F32, name="score%d_%d" % (g, b)) for b in range(SCORE_BANKS[g])] for g in range(2)]
        out_bank = [ps.tile([P, 512], F32, name="y%d" % b) for b in range(2)]
        bank_turn = [0, 0]

        def pair_rows(x, g):
            return x[2 * g : 2 * g + 2].rearrange("h (p j) n -> (h p) j n", j=PACK)

        raw = {}

        def load(name, src):
            raw[name] = new("raw_" + name, list(src.shape), F32)
            nc.sync.dma_start(out=raw[name][:], in_=src)

        t_col = new("t_col", [P, PACK], F32)
        t_rep = new("t_rep", [P, PACK, 4], F32)
        kb_col = new("kb_col", [P, PACK], F32)
        kb_half = new("kb_half", [P, PACK], F32)
        warm = new("warm", [P, 1], F32)
        warm_out = new("warm_out", [P, 1], F32)

        k_bf = [new("k_bf%d" % g, [P, PACK, P, PACK], BF16) for g in range(2)]
        q_bf = [new("q_bf%d" % g, [P, NQ, PACK], BF16) for g in range(2)]
        v_bf = new("v_bf", [P, H, E, PACK], BF16)
        codes = {}
        scales = {}

        def copy(engine, dst, src):
            if engine == "V":
                nc.vector.tensor_copy(out=dst, in_=src)
            else:
                nc.scalar.copy(out=dst, in_=src)

        def cast_k(engine, g, name, s0, a, b):
            copy(engine,
                 k_bf[g][:, :, s0 + a : s0 + b, :].rearrange("p r s j -> p s j r"),
                 raw[name][:, :, PACK * a : PACK * b].rearrange("p j (s r) -> p s j r", r=PACK))

        def cast_q(engine, g, name, q0, a, b):
            copy(engine,
                 q_bf[g][:, q0 + a : q0 + b, :].rearrange("p (c i) j -> p c j i", i=4),
                 raw[name][:, :, a:b].rearrange("p j (c i) -> p c j i", i=4))

        def cast_v(engine, name, h0, h1):
            copy(engine,
                 v_bf[:, h0:h1].rearrange("p h (c i) j -> p h c j i", i=4),
                 raw[name][:].rearrange("p h j (c i) -> p h c j i", i=4))

        def quantize(name, src, width):
            cd = new("codes_" + name, [P, width], U32)
            sc = new("scales_" + name, [P, width], U8)
            nc.vector.quantize_mx(out=cd[:].bitcast(FP8X4), scales=sc[:], in_=src)
            return cd, sc

        def quant_k(g, r0, r1):
            cd, sc = quantize("k%d_%d" % (g, r0), k_bf[g][:, r0:r1].rearrange("p r s j -> p (r s j)"), (r1 - r0) * P)
            for r in range(r0, r1):
                codes["k", g, r] = cd[:, (r - r0) * P : (r - r0 + 1) * P]
                scales["k", g, r] = sc[:, (r - r0) * P : (r - r0 + 1) * P]

        def quant_q(g, c0, c1):
            cd, sc = quantize("q%d_%d" % (g, c0), q_bf[g][:, c0 * CH : c1 * CH].rearrange("p q j -> p (q j)"), (c1 - c0) * CH)
            for c in range(c0, c1):
                codes["q", g, c] = cd[:, (c - c0) * CH : (c - c0 + 1) * CH]
                scales["q", g, c] = sc[:, (c - c0) * CH : (c - c0 + 1) * CH]

        def quant_v(h0, h1):
            cd, sc = quantize("v%d" % h0, v_bf[:, h0:h1].rearrange("p h e j -> p (h e j)"), (h1 - h0) * E)
            for h in range(h0, h1):
                codes["v", h] = cd[:, (h - h0) * E : (h - h0 + 1) * E]
                scales["v", h] = sc[:, (h - h0) * E : (h - h0 + 1) * E]

        capped = {}
        prob = {}
        w_bf = [new("w%d" % h, [P, NQ, PACK], BF16) for h in range(H)]

        def scores(*jobs):
            passes = []
            reads = []
            for h, c0, c1, r0, r1 in jobs:
                g, x = divmod(h, 2)
                rows = slice(ROWS * x, ROWS * (x + 1))
                nq = (c1 - c0) * CH
                if (h, c0) not in capped:
                    u = new("u%d_%d" % (h, c0), [P, PACK, nq], F32)
                    for c in range(c0, c1):
                        capped[h, c] = (u, c0)
                bank = score_bank[x][bank_turn[x] % SCORE_BANKS[x]]
                bank_turn[x] = bank_turn[x] + 1
                passes.append([(bank, (r - r0) * nq + (c - c0) * CH, rows, ("k", g, r), ("q", g, c))
                               for r in range(r0, r1) for c in range(c0, c1)])
                reads.extend([(capped[h, c0][0], r, bank, (r - r0) * nq, nq) for r in range(r0, r1)])
            for step in zip(*passes):
                for bank, col, rows, keys, queries in step:
                    nc.tensor.matmul_mx(
                        out=bank[:, col : col + CH],
                        lhsT=codes[keys][rows, :].bitcast(FP8X4),
                        lhsT_scale=scales[keys][rows, :],
                        rhs=codes[queries][rows, :].bitcast(FP8X4),
                        rhs_scale=scales[queries][rows, :],
                        start=True,
                        stop=True,
                    )
            for u, r, bank, col, nq in reads:
                nc.scalar.activation(out=u[:, r, :], in_=bank[:, col : col + nq], func=ACT.Tanh,
                                     bias=kb_half[:, r : r + 1], scale=0.5)

        def sigmoid(h, c0, c1):
            u, base = capped[h, c0]
            pr = new("p%d_%d" % (h, c0), [P, PACK, (c1 - c0) * CH], F32)
            for c in range(c0, c1):
                prob[h, c] = (pr, c0)
            nc.scalar.activation(out=pr[:], in_=u[:, :, (c0 - base) * CH : (c1 - base) * CH], func=ACT.Sigmoid, scale=2.0)

        def weigh(h, c0, c1):
            pr, base = prob[h, c0]
            nq = (c1 - c0) * CH
            nc.vector.tensor_tensor(
                out=w_bf[h][:, c0 * CH : c1 * CH].rearrange("p (c i) r -> p c r i", i=4),
                in0=pr[:, :, (c0 - base) * CH : (c1 - base) * CH].rearrange("p r (c i) -> p c r i", i=4),
                in1=t_rep[:].unsqueeze(1).to_broadcast([P, nq // 4, PACK, 4]),
                op=ALU.mult,
            )

        def quant_w(h, c0, c1):
            cd, sc = quantize("w%d_%d" % (h, c0), w_bf[h][:, c0 * CH : c1 * CH].rearrange("p q r -> p (q r)"), (c1 - c0) * CH)
            for c in range(c0, c1):
                codes["w", h, c] = cd[:, (c - c0) * CH : (c - c0 + 1) * CH]
                scales["w", h, c] = sc[:, (c - c0) * CH : (c - c0 + 1) * CH]

        def values(h, c0, c1, b, base):
            for c in range(c0, c1):
                nc.tensor.matmul_mx(
                    out=out_bank[b][:, (c - base) * E : (c - base + 1) * E],
                    lhsT=codes["w", h, c].bitcast(FP8X4),
                    lhsT_scale=scales["w", h, c],
                    rhs=codes["v", h].bitcast(FP8X4),
                    rhs_scale=scales["v", h],
                    start=True,
                    stop=True,
                )

        def finish(engine, h, c0, c1, b, base, queue=None):
            n = c1 - c0
            y = new("y%d_%d" % (h, c0), [P, n * E], F32)
            if engine == "V":
                nc.vector.tensor_scalar(out=y[:], in0=out_bank[b][:, (c0 - base) * E : (c1 - base) * E], scalar1=1.0 / 16.0, scalar2=None, op0=ALU.mult)
            else:
                nc.scalar.activation(out=y[:], in_=out_bank[b][:, (c0 - base) * E : (c1 - base) * E], func=ACT.Copy, scale=1.0 / 16.0)
            (queue or nc.sync).dma_start(
                out=out[h, c0 * CH : c1 * CH, :].rearrange("(c m) e -> m c e", m=P),
                in_=y[:].rearrange("p (c e) -> p c e", e=E),
            )

        nc.scalar.dma_start(out=kb_col[:], in_=kb.rearrange("(p r) o -> p (r o)", r=PACK))
        nc.vector.memset(warm[:], 0.0)
        nc.scalar.activation(out=warm_out[:], in_=warm[:], func=ACT.Sigmoid)
        load("k0", pair_rows(kT, 0))
        load("q0a", pair_rows(qT, 0)[:, :, 0:128])
        load("q0b", pair_rows(qT, 0)[:, :, 128:512])
        nc.sync.dma_start(out=t_col[:], in_=t.rearrange("(p r) o -> p (r o)", r=PACK))
        load("k1", pair_rows(kT, 1))
        load("q1", pair_rows(qT, 1))
        load("va", v[0:2].rearrange("h (p j) e -> p h j e", j=PACK))
        load("vb", v[2:4].rearrange("h (p j) e -> p h j e", j=PACK))
        nc.vector.tensor_scalar(out=kb_half[:], in0=kb_col[:], scalar1=0.5, scalar2=None, op0=ALU.mult)
        cast_k("V", 0, "k0", 0, 0, 88)
        cast_k("S", 0, "k0", 0, 88, 128)
        cast_q("V", 0, "q0a", 0, 0, 128)
        quant_k(0, 0, 1)
        quant_q(0, 0, 1)
        quant_k(0, 1, 2)
        quant_k(0, 2, 4)
        scores((0, 0, 1, 0, 1), (1, 0, 1, 0, 1))
        scores((0, 0, 1, 1, 2), (1, 0, 1, 1, 2))
        scores((0, 0, 1, 2, 4), (1, 0, 1, 2, 4))
        cast_q("V", 0, "q0b", 128, 0, 128)
        cast_q("V", 0, "q0b", 128, 128, 384)
        quant_q(0, 1, 2)
        nc.vector.tensor_copy(out=t_rep[:], in_=t_col[:].unsqueeze(2).to_broadcast([P, PACK, 4]))
        quant_q(0, 2, 4)
        sigmoid(0, 0, 1)
        sigmoid(1, 0, 1)
        scores((0, 1, 4, 0, 1), (1, 1, 4, 0, 1))
        scores((0, 1, 4, 1, 2), (1, 1, 4, 1, 2))
        scores((0, 1, 4, 2, 3), (1, 1, 4, 2, 3))
        scores((0, 1, 4, 3, 4), (1, 1, 4, 3, 4))
        weigh(0, 0, 1)
        cast_k("V", 1, "k1", 0, 0, 128)
        weigh(1, 0, 1)
        cast_q("V", 1, "q1", 0, 0, 512)
        quant_k(1, 0, 4)
        quant_q(1, 0, 4)
        sigmoid(0, 1, 4)
        sigmoid(1, 1, 4)
        cast_v("V", "va", 0, 2)
        cast_v("V", "vb", 2, 4)
        weigh(0, 1, 4)
        quant_v(0, 4)
        quant_w(0, 0, 4)
        scores((2, 0, 4, 0, 1),)
        scores((2, 0, 4, 1, 2),)
        scores((2, 0, 4, 2, 3), (3, 0, 2, 0, 2))
        scores((2, 0, 4, 3, 4), (3, 0, 2, 2, 4))
        values(0, 0, 4, 0, 0)
        weigh(1, 1, 4)
        finish("V", 0, 0, 4, 0, 0)
        quant_w(1, 0, 4)
        sigmoid(2, 0, 2)
        sigmoid(2, 2, 4)
        sigmoid(3, 0, 2)
        scores((3, 2, 4, 0, 2),)
        scores((3, 2, 4, 2, 4),)
        values(1, 0, 4, 1, 0)
        weigh(2, 0, 2)
        weigh(2, 2, 4)
        quant_w(2, 0, 2)
        weigh(3, 0, 2)
        quant_w(2, 2, 4)
        finish("S", 1, 0, 4, 1, 0)
        sigmoid(3, 2, 3)
        sigmoid(3, 3, 4)
        values(2, 0, 4, 0, 0)
        quant_w(3, 0, 2)
        values(3, 0, 2, 1, 0)
        finish("S", 2, 0, 4, 0, 0)
        finish("S", 3, 0, 2, 1, 0)
        weigh(3, 2, 3)
        weigh(3, 3, 4)
        quant_w(3, 2, 3)
        quant_w(3, 3, 4)
        values(3, 2, 3, 0, 2)
        values(3, 3, 4, 1, 3)
        finish("V", 3, 2, 3, 0, 2)
        finish("S", 3, 3, 4, 1, 3, nc.scalar)
